import numpy as np
import ml_dtypes


def mxq(x, axis, fmt="e4m3"):
    dtype, down = {"e4m3": (ml_dtypes.float8_e4m3fn, 7), "e5m2": (ml_dtypes.float8_e5m2, 14)}[fmt]
    v = np.moveaxis(np.asarray(x, np.float32).astype(ml_dtypes.bfloat16).astype(np.float64), axis, -1)
    blocks = v.reshape(v.shape[:-1] + (-1, 32))
    amax = np.abs(blocks).max(-1, keepdims=True)
    byte = np.maximum(np.where(amax > 0, np.frexp(amax)[1] - 1 + 127, 0) - down, 1)
    scale = np.exp2(byte - 127.0)
    codes = (blocks / scale).astype(np.float32).astype(dtype).astype(np.float64)
    return np.moveaxis((codes * scale).reshape(v.shape), -1, axis)


WIDE = False


def mx_kscale(k):
    if not WIDE:
        return np.ones(k)
    levels = np.array([10, -10, 5, -5, 0])
    if k % 512:
        return np.exp2(np.random.permutation(np.resize(levels, k // 32))).repeat(32)
    a = np.empty((k // 512, 16))
    for p in range(k // 512):
        a[p, :8] = np.random.permutation(np.resize(levels, 8))
        for g in range(8):
            far = levels[np.abs(levels - a[p, g]) >= 10]
            a[p, g + 8] = far[np.random.randint(len(far))]
    return np.exp2(a.ravel()).repeat(32)


BF16 = ml_dtypes.bfloat16


def bf(x):
    return np.asarray(x, np.float32).astype(BF16)


def f64(x):
    return np.asarray(x).astype(np.float64)


E2M1 = np.array([0.0, 0.5, 1.0, 1.5, 2.0, 3.0, 4.0, 6.0, -0.0, -0.5, -1.0, -1.5, -2.0, -3.0, -4.0, -6.0])


def pack_weight(w, fmt):
    k, n = w.shape
    w = f64(bf(w)).reshape(k // 32, 32, n)
    amax = np.abs(w).max(1)
    if fmt == "e4m3":
        byte = np.frexp(amax)[1] - 1 + 127 - 7
    else:
        mant, ex = np.frexp(amax / 6.0)
        byte = np.where(mant > 0.5, ex, ex - 1) + 127
    byte = np.clip(np.where(amax > 0, byte, 1), 1, 254)
    scaled = (w * np.exp2(127.0 - byte)[:, None, :]).reshape(k, n).astype(np.float32)
    by_word = np.ascontiguousarray(scaled.reshape(k // 512, 128, 4, n).transpose(0, 1, 3, 2))
    if fmt == "e4m3":
        words = by_word.astype(ml_dtypes.float8_e4m3fn).view(np.uint8)
    else:
        c = by_word.astype(ml_dtypes.float4_e2m1fn).view(np.uint8) & 0xF
        words = c[..., 0::2] | (c[..., 1::2] << 4)
    return np.ascontiguousarray(words), np.ascontiguousarray(byte.astype(np.uint8).reshape(k // 512, 16, n))


def unpack_weight(words, scales, fmt):
    g, p, n, _ = words.shape
    if fmt == "e4m3":
        vals = np.ascontiguousarray(words).view(ml_dtypes.float8_e4m3fn).astype(np.float64)
    else:
        nib = np.empty((g, p, n, 4), np.uint8)
        nib[..., 0::2] = words & 0xF
        nib[..., 1::2] = words >> 4
        vals = E2M1[nib]
    vals = vals * np.repeat(np.exp2(scales.astype(np.float64) - 127.0), 8, axis=1)[..., None]
    return vals.transpose(0, 1, 3, 2).reshape(g * 512, n)
def pack4(w):
    words, scales = pack_weight(w, "e2m1")
    return words.reshape(words.shape[0], 128, -1), scales


def unpack4(words, scales):
    return unpack_weight(words.reshape(words.shape[0], 128, -1, 2), scales, "e2m1")


E4M3FN = np.array([(-1.0 if i & 128 else 1.0) * ((1.0 + (i & 7) / 8.0) * 2.0 ** (((i >> 3) & 15) - 7) if i & 120 else (i & 7) * 2.0 ** -9) for i in range(256)])


def e4m3fn_bytes(y):
    return np.clip(np.asarray(y, np.float64), -448.0, 448.0).astype(np.float32).astype(ml_dtypes.float8_e4m3fn).view(np.uint8)


def e4m3fn_values(b):
    return E4M3FN[b]


T, H, C, O = 1024, 512, 1024, 1024


def draw0():
    s = mx_kscale(H)
    t = mx_kscale(C)
    c = np.random.standard_normal((T, H)) * s
    q = np.random.standard_normal((T, C))
    wm = np.random.standard_normal((H, C)) / np.sqrt(H) / s[:, None]
    wl = np.random.standard_normal((H, C)) / np.sqrt(H) / s[:, None]
    wq = np.random.standard_normal((C, C)) / np.sqrt(C)
    ig = (1.0 + 0.1 * np.random.standard_normal(C)) * t
    ws = np.random.standard_normal((C, O)) / np.sqrt(C) / t[:, None]
    wm_words, wm_scales = pack4(wm)
    wl_words, wl_scales = pack4(wl)
    ws_words, ws_scales = pack4(ws)
    return {"c": bf(c), "q": bf(q), "wm_words": wm_words, "wm_scales": wm_scales, "wl_words": wl_words, "wl_scales": wl_scales, "wq": bf(wq), "ig": bf(ig), "ws_words": ws_words, "ws_scales": ws_scales}


def latent_residual_prediction(cq, q, wl_words, wl_scales, wq):
    l = (cq @ unpack4(wl_words, wl_scales)) + f64(q) @ f64(wq)
    return 0.5 * np.tanh(l)


def core(c, q, wm_words, wm_scales, wl_words, wl_scales, wq, ig, ws_words, ws_scales):
    cq = mxq(f64(c), 1, "e4m3")
    mu = cq @ unpack4(wm_words, wm_scales)
    r = latent_residual_prediction(cq, q, wl_words, wl_scales, wq)
    y = f64(q) + mu + r
    yg = f64(ig)[None, :] * y
    return mxq(yg, 1, "e4m3") @ unpack4(ws_words, ws_scales)


def setup_inputs():
    drawn = draw0()
    full = np.asarray(drawn['c']).astype(np.float64)
    scale = (np.abs(full).reshape(1024, 4, 128).max(axis=(2,)) / 448.0).astype(np.float32)
    given = {}
    for key, value in drawn.items():
        if key == 'c':
            given['c_bytes'] = e4m3fn_bytes(full / np.repeat(scale.astype(np.float64), 128, axis=1))
            given['c_scale'] = scale
        else:
            given[key] = value
    return given


def reference(c_bytes, c_scale, q, wm_words, wm_scales, wl_words, wl_scales, wq, ig, ws_words, ws_scales):
    return core(e4m3fn_values(c_bytes) * np.repeat(c_scale.astype(np.float64), 128, axis=1), q, wm_words, wm_scales, wl_words, wl_scales, wq, ig, ws_words, ws_scales)

@@ -1,0 +1,416 @@
+from contextlib import ExitStack
+
+import concourse.mybir as mybir
+from concourse.masks import make_identity
+
+T, H, C, O = 1024, 512, 1024, 1024
+FLOPS = 2 * T * H * C * 2 + 2 * T * C * C + 2 * T * C * O
+
+F32 = mybir.dt.float32
+BF16 = mybir.dt.bfloat16
+I32 = mybir.dt.int32
+U32 = mybir.dt.uint32
+U8 = mybir.dt.uint8
+FP8 = mybir.dt.float8_e4m3fn
+FP8X4 = mybir.dt.float8_e4m3fn_x4
+FP4X4 = mybir.dt.float4_e2m1fn_x4
+ADD = mybir.AluOpType.add
+MULT = mybir.AluOpType.mult
+COPY = mybir.ActivationFunctionType.Copy
+TANH = mybir.ActivationFunctionType.Tanh
+
+P = 128
+
+
+def tile_inversegainlatentresidualpredictionsynth_d1p_kernel(
+    tc, c_bytes, c_scale, q, wm_words, wm_scales, wl_words, wl_scales, wq, ig, ws_words, ws_scales, out
+):
+    nc = tc.nc
+    with ExitStack() as ctx:
+        keep = ctx.enter_context(tc.tile_pool(name="keep", bufs=1))
+        work = ctx.enter_context(tc.tile_pool(name="work", bufs=3))
+        psum = ctx.enter_context(tc.psum_pool(name="psum", bufs=8))
+        ctx.enter_context(tc.manual_schedule())
+
+        ident = keep.tile([P, P], F32, name="ident")
+        make_identity(nc, ident[:])
+        c8 = [keep.tile([P, 4, 512], U8, name="c8_0"), keep.tile([P, 4, 512], U8, name="c8_1")]
+        csc = keep.tile([P, 32], F32, name="csc")
+        igb = keep.tile([P, 8], BF16, name="igb")
+        qs = [[keep.tile([P, 2, 1024], BF16, name="qs00"), keep.tile([P, 2, 1024], BF16, name="qs01")],
+              [keep.tile([P, 2, 1024], BF16, name="qs10"), keep.tile([P, 2, 1024], BF16, name="qs11")]]
+        wqs = [keep.tile([P, 2, 4, 512], BF16, name="wqs0"), keep.tile([P, 2, 4, 512], BF16, name="wqs1")]
+        wl_w = keep.tile([P, 2048], U8, name="wl_w")
+        wm_w = keep.tile([P, 2048], U8, name="wm_w")
+        wl_sr = keep.tile([P, 1024], U8, name="wl_sr")
+        wm_sr = keep.tile([P, 1024], U8, name="wm_sr")
+        ws_w = keep.tile([P, 2, 2048], U8, name="ws_w", align_bytes=64)
+        ws_s = keep.tile([P, 2, 1024], U8, name="ws_s", align_bytes=64)
+
+        nc.vector.memset(wl_sr[:].bitcast(I32), 0)
+        nc.vector.memset(wm_sr[:].bitcast(I32), 0)
+        nc.vector.memset(ws_s[:].rearrange("p g n -> p (g n)").bitcast(I32), 0)
+
+        cb_v = c_bytes.rearrange("(p i) k -> p i k", i=8)
+        q_v = q.rearrange("(p i) c -> p i c", i=8)
+        wq_v = wq.rearrange("(g p t) c -> g p t c", p=P, t=4)
+        nc.sync.dma_start(out=csc[:], in_=c_scale.rearrange("(p i) j -> p (i j)", i=8))
+        nc.sync.dma_start(out=c8[0][:], in_=cb_v[:, 0:4, :])
+        nc.sync.dma_start(out=qs[0][0][:], in_=q_v[:, 0:2, :])
+        nc.sync.dma_start(out=qs[0][1][:], in_=q_v[:, 2:4, :])
+        for qd in range(4):
+            rows = slice(32 * qd, 32 * qd + 4)
+            nc.scalar.dma_start(out=wl_sr[rows, :].bitcast(I32), in_=wl_scales[0, 4 * qd : 4 * qd + 4, :].bitcast(I32))
+            nc.gpsimd.dma_start(out=wm_sr[rows, :].bitcast(I32), in_=wm_scales[0, 4 * qd : 4 * qd + 4, :].bitcast(I32))
+        nc.sync.dma_start(out=igb[:], in_=ig.rearrange("(g p t) -> p g t", p=P, t=4))
+        for gk in range(2):
+            nc.sync.dma_start(out=wqs[0][:, gk, :, :], in_=wq_v[gk, :, :, 0:512])
+        nc.sync.dma_start(out=wl_w[:].bitcast(I32), in_=wl_words[0].bitcast(I32))
+        nc.sync.dma_start(out=wm_w[:].bitcast(I32), in_=wm_words[0].bitcast(I32))
+        nc.sync.dma_start(out=c8[1][:], in_=cb_v[:, 4:8, :])
+        for gk in range(2):
+            nc.sync.dma_start(out=wqs[1][:, gk, :, :], in_=wq_v[gk, :, :, 512:1024])
+        nc.sync.dma_start(out=qs[1][0][:], in_=q_v[:, 4:6, :])
+        nc.sync.dma_start(out=qs[1][1][:], in_=q_v[:, 6:8, :])
+        for g in range(2):
+            nc.sync.dma_start(out=ws_w[:, g, :].bitcast(I32), in_=ws_words[g].bitcast(I32))
+        for qd in range(4):
+            for g in range(2):
+                nc.sync.dma_start(
+                    out=ws_s[32 * qd : 32 * qd + 4, g, :].bitcast(I32),
+                    in_=ws_scales[g, 4 * qd : 4 * qd + 4, :].bitcast(I32),
+                )
+
+        warm = keep.tile([P, 1], F32, name="warm")
+        nc.scalar.activation(out=warm[:], in_=ident[:, 0:1], func=TANH)
+        igf = keep.tile([P, 8], F32, name="igf")
+        igh = keep.tile([P, 8], F32, name="igh")
+
+        qt = [keep.tile([P, 2, 2, 512], F32, name="qt0"), keep.tile([P, 2, 2, 512], F32, name="qt1")]
+        cbf = keep.tile([P, 8, 512], BF16, name="cbf")
+        cq = [keep.tile([P, 512], U32, name="cq0", align_bytes=64), keep.tile([P, 512], U32, name="cq1", align_bytes=64)]
+        cqs = [keep.tile([P, 512], U8, name="cqs0", align_bytes=64), keep.tile([P, 512], U8, name="cqs1", align_bytes=64)]
+        wl_p = keep.tile([P, 2048], U8, name="wl_p", align_bytes=64)
+        wm_p = keep.tile([P, 2048], U8, name="wm_p", align_bytes=64)
+        wl_sp = keep.tile([P, 1024], U8, name="wl_sp", align_bytes=64)
+        wm_sp = keep.tile([P, 1024], U8, name="wm_sp", align_bytes=64)
+        yq = [keep.tile([P, 2, 512], U32, name="yq0", align_bytes=64), keep.tile([P, 2, 512], U32, name="yq1", align_bytes=64)]
+        yqs = [keep.tile([P, 2, 512], U8, name="yqs0", align_bytes=64), keep.tile([P, 2, 512], U8, name="yqs1", align_bytes=64)]
+
+        def widen(h, i, on_scalar):
+            for j in range(4):
+                ks = slice(128 * j, 128 * j + 128)
+                src = c8[h][:, i, ks].bitcast(FP8)
+                col = csc[:, 4 * (4 * h + i) + j : 4 * (4 * h + i) + j + 1]
+                dst = cbf[:, 4 * h + i, ks]
+                if on_scalar:
+                    nc.scalar.activation(out=dst, in_=src, func=COPY, scale=col)
+                else:
+                    nc.vector.tensor_scalar(out=dst, in0=src, scalar1=col, scalar2=None, op0=MULT)
+
+        def copy(on_scalar, dst, src):
+            if on_scalar:
+                nc.scalar.copy(out=dst, in_=src)
+            else:
+                nc.vector.tensor_copy(out=dst, in_=src)
+
+        grp = {}
+
+        def c_turn(h, pair, on_scalar):
+            bank = psum.tile([P, 2, 2, 128], F32, name="bank", tag="bank")
+            for j in range(2):
+                words = cbf[:, 4 * h + 2 * pair + j, :].bitcast(F32)
+                for u in range(2):
+                    nc.tensor.transpose(bank[:, u, j, :], words[:, u : 256 : 2], ident[:])
+            if pair == 0:
+                grouped = work.tile([P, 512, 4], BF16, name="grouped", align_bytes=64)
+                grp[h] = grouped
+            dst = grp[h][:].rearrange("p n t -> p (n t)").bitcast(F32).rearrange("p (n u) -> p n u", u=2)
+            copy(on_scalar, dst[:, 256 * pair : 256 * pair + 256, :], bank[:].rearrange("p u j n -> p (j n) u"))
+
+        def c_quant(h):
+            nc.vector.quantize_mx(
+                out=cq[h][:].bitcast(FP8X4), scales=cqs[h][:], in_=grp[h][:].rearrange("p n t -> p (n t)")
+            )
+
+        def q_turn(h, pair, g, on_scalar):
+            bank = psum.tile([P, 2, 2, 128], F32, name="bank", tag="bank")
+            for j in range(2):
+                words = qs[h][pair][:, j, :].bitcast(F32)
+                for u in range(2):
+                    nc.tensor.transpose(bank[:, u, j, :], words[:, 256 * g + u : 256 * g + 256 : 2], ident[:])
+            copy(
+                on_scalar,
+                qt[h][:, g, :, 256 * pair : 256 * pair + 256],
+                bank[:].rearrange("p u j n -> p u (j n)"),
+            )
+
+        def qt_view(h, g, t):
+            return qt[h][:, g, t // 2, :].bitcast(BF16)[:, t % 2 : 1024 : 2]
+
+        def permute_words(g, eng):
+            b = slice(1024 * g, 1024 * g + 1024)
+            for src, dst in ((wl_w, wl_p), (wm_w, wm_p)):
+                eng.tensor_copy(
+                    out=dst[:, b].rearrange("p (t m b) -> p t m b", t=4, b=2),
+                    in_=src[:, b].rearrange("p (m t b) -> p t m b", t=4, b=2),
+                )
+
+        def permute_scales(g):
+            b = slice(512 * g, 512 * g + 512)
+            for src, dst in ((wl_sr, wl_sp), (wm_sr, wm_sp)):
+                nc.gpsimd.tensor_copy(
+                    out=dst[:, b].rearrange("p (t m) -> p t m", t=4),
+                    in_=src[:, b].rearrange("p (m t) -> p t m", t=4),
+                )
+
+        units = [(0, 0), (0, 1), (1, 0), (1, 1)]
+        st = {}
+
+        def pl(u, t, n0=0, n1=512):
+            h, g = units[u]
+            bank = psum.tile([P, n1 - n0], F32, name="bank", tag="bank")
+            st["pl", u, t, n0] = bank
+            n = 0
+            for gk in range(2):
+                for tk in range(4):
+                    nc.tensor.matmul(
+                        bank[:],
+                        lhsT=wqs[g][:, gk, tk, t : 512 : 4],
+                        rhs=qt_view(h, gk, tk)[:, n0:n1],
+                        start=(n == 0),
+                        stop=(n == 7),
+                    )
+                    n += 1
+
+        def mx1(u, t, wp, wsp, key):
+            h, g = units[u]
+            k = 4 * g + t
+            bank = psum.tile([P, 512], F32, name="bank", tag="bank")
+            st[key, u, t] = bank
+            nc.tensor.matmul_mx(
+                out=bank[:],
+                lhsT=wp[:, 256 * k : 256 * k + 256].bitcast(FP4X4),
+                lhsT_scale=wsp[:, 128 * k : 128 * k + 128],
+                rhs=cq[h][:].bitcast(FP8X4),
+                rhs_scale=cqs[h][:],
+                start=True,
+                stop=True,
+            )
+
+        def igq(u, t):
+            h, g = units[u]
+            z = work.tile([P, 512], F32, name="igqt", bufs=5)
+            st["igq", u, t] = z
+            nc.scalar.activation(out=z[:], in_=qt_view(h, g, t), func=COPY, scale=igf[:, 4 * g + t : 4 * g + t + 1])
+
+        def mx_pair(u, t):
+            mx1(u, t, wl_p, wl_sp, "mxl")
+            mx1(u, t, wm_p, wm_sp, "mxm")
+
+        def a_op(u, t):
+            z = work.tile([P, 512], F32, name="lmx", bufs=5)
+            st["lmx", u, t] = z
+            nc.scalar.copy(out=z[:], in_=st["mxl", u, t][:])
+
+        def d_op(u, t):
+            g = units[u][1]
+            z = work.tile([P, 512], F32, name="wsum", bufs=5)
+            st["w", u, t] = z
+            nc.vector.scalar_tensor_tensor(
+                out=z[:], in0=st["mxm", u, t][:], scalar=igf[:, 4 * g + t : 4 * g + t + 1], in1=st["igq", u, t][:],
+                op0=MULT, op1=ADD,
+            )
+
+        def b_op(u, t, n0=0, n1=512):
+            z = work.tile([P, n1 - n0], F32, name="lsum", bufs=3)
+            st["ls", u, t, n0] = z
+            nc.vector.tensor_tensor(out=z[:], in0=st["pl", u, t, n0][:], in1=st["lmx", u, t][:, n0:n1], op=ADD)
+
+        def c_op(u, t, n0=0, n1=512):
+            z = work.tile([P, n1 - n0], F32, name="th", bufs=3)
+            st["th", u, t, n0] = z
+            nc.scalar.activation(out=z[:], in_=st["ls", u, t, n0][:], func=TANH)
+
+        def e_op(u, t, n0=0, n1=512):
+            g = units[u][1]
+            if t == 0 and n0 == 0:
+                ye = work.tile([P, 4, 512], BF16, name="ye", bufs=2)
+                st["ye", u] = ye
+            nc.vector.scalar_tensor_tensor(
+                out=st["ye", u][:, t, n0:n1], in0=st["th", u, t, n0][:], scalar=igh[:, 4 * g + t : 4 * g + t + 1],
+                in1=st["w", u, t][:, n0:n1], op0=MULT, op1=ADD,
+            )
+
+        def f_op(u, n0, n1):
+            if n0 == 0:
+                yi = work.tile([P, 512, 4], BF16, name="yi", bufs=2, align_bytes=64)
+                st["yi", u] = yi
+            nc.vector.tensor_copy(
+                out=st["yi", u][:, n0:n1, :], in_=st["ye", u][:, :, n0:n1].rearrange("p t n -> p n t")
+            )
+
+        def q_op(u, n0, n1):
+            h, g = units[u]
+            nc.vector.quantize_mx(
+                out=yq[h][:, g, n0:n1].bitcast(FP8X4),
+                scales=yqs[h][:, g, n0:n1],
+                in_=st["yi", u][:, n0:n1, :].rearrange("p n t -> p (n t)"),
+            )
+
+        out_v = out.rearrange("(p i) o -> p i o", i=8)
+
+        def st2(h, i, o):
+            bank = psum.tile([P, 512], F32, name="bank", tag="bank")
+            st["o", h, i, o] = bank
+            for g in range(2):
+                nc.tensor.matmul_mx(
+                    out=bank[:],
+                    lhsT=yq[h][:, g, 128 * i : 128 * i + 128].bitcast(FP8X4),
+                    lhsT_scale=yqs[h][:, g, 128 * i : 128 * i + 128],
+                    rhs=ws_w[:, g, 1024 * o : 1024 * o + 1024].bitcast(FP4X4),
+                    rhs_scale=ws_s[:, g, 512 * o : 512 * o + 512],
+                    start=(g == 0),
+                    stop=(g == 1),
+                )
+
+        def o_op(h, i, o, on_scalar):
+            ot = work.tile([P, 512], F32, name="ot", bufs=10)
+            copy(on_scalar, ot[:], st["o", h, i, o][:])
+            nc.sync.dma_start(out=out_v[:, 4 * h + i, 512 * o : 512 * o + 512], in_=ot[:])
+
+        widen(0, 0, False)
+        widen(0, 1, True)
+        widen(0, 2, False)
+        widen(0, 3, True)
+        c_turn(0, 0, False)
+        c_turn(0, 1, True)
+        q_turn(0, 0, 0, False)
+        q_turn(0, 0, 1, True)
+        c_quant(0)
+        q_turn(0, 1, 0, False)
+        q_turn(0, 1, 1, True)
+        nc.vector.tensor_copy(out=igf[:], in_=igb[:])
+        nc.vector.tensor_scalar(out=igh[:], in0=igb[:], scalar1=0.5, scalar2=None, op0=MULT)
+        for t in range(4):
+            igq(0, t)
+        permute_scales(0)
+        permute_scales(1)
+        permute_words(0, nc.vector)
+        permute_words(1, nc.gpsimd)
+        for i in range(4):
+            widen(1, i, i % 2 == 1)
+        pl(0, 0)
+        pl(0, 1)
+        mx_pair(0, 0)
+        a_op(0, 0)
+        d_op(0, 0)
+        mx_pair(0, 1)
+        a_op(0, 1)
+        b_op(0, 0)
+        c_op(0, 0)
+        d_op(0, 1)
+        b_op(0, 1)
+        c_op(0, 1)
+        e_op(0, 0)
+        pl(0, 2)
+        mx_pair(0, 2)
+        a_op(0, 2)
+        e_op(0, 1)
+        b_op(0, 2)
+        d_op(0, 2)
+        c_op(0, 2)
+        igq(1, 0)
+        pl(0, 3)
+        mx_pair(0, 3)
+        a_op(0, 3)
+        e_op(0, 2)
+        b_op(0, 3)
+        d_op(0, 3)
+        c_op(0, 3)
+        slots = [(u, t) for u in (1, 2) for t in range(4)]
+        extra = {
+            (1, 0): [lambda: c_turn(1, 0, False), lambda: c_turn(1, 1, True)],
+            (1, 1): [lambda: q_turn(1, 0, 0, False), lambda: q_turn(1, 0, 1, True)],
+            (1, 2): [lambda: c_quant(1), lambda: q_turn(1, 1, 0, False), lambda: q_turn(1, 1, 1, True)],
+        }
+        plan = {(2, 2): [(0, 0), (0, 1)], (2, 3): [(1, 0), (1, 1), (2, 0)]}
+        for s, (u, t) in enumerate(slots):
+            pu, pt = (u, t - 1) if t else (u - 1, 3)
+            mx_pair(u, t)
+            a_op(u, t)
+            if s:
+                b_op(pu, pt)
+                c_op(pu, pt)
+            d_op(u, t)
+            e_op(pu, pt)
+            for f in extra.get((u, t), []):
+                f()
+            for i, o in plan.get((u, t), []):
+                st2(0, i, o)
+            pl(u, t)
+            igq(*((u, t + 1) if t < 3 else (u + 1, 0)))
+            for i, o in plan.get((u, t), []):
+                o_op(0, i, o, True)
+            if t == 0:
+                f_op(u - 1, 0, 512)
+                q_op(u - 1, 0, 512)
+        for t in range(4):
+            mx_pair(3, t)
+            a_op(3, t)
+            if t == 0:
+                b_op(2, 3)
+                c_op(2, 3)
+            else:
+                b_op(3, t - 1, 0, 256)
+                c_op(3, t - 1, 0, 256)
+            d_op(3, t)
+            if t == 0:
+                e_op(2, 3)
+            else:
+                e_op(3, t - 1, 0, 256)
+            if t < 3:
+                igq(3, t + 1)
+            if t == 1:
+                f_op(2, 0, 512)
+                q_op(2, 0, 512)
+            pl(3, t, 0, 256)
+        pl(3, 0, 256, 512)
+        b_op(3, 3, 0, 256)
+        c_op(3, 3, 0, 256)
+        st2(0, 2, 1)
+        o_op(0, 2, 1, True)
+        pl(3, 1, 256, 512)
+        b_op(3, 0, 256, 512)
+        e_op(3, 3, 0, 256)
+        c_op(3, 0, 256, 512)
+        f_op(3, 0, 256)
+        st2(0, 3, 0)
+        o_op(0, 3, 0, True)
+        pl(3, 2, 256, 512)
+        b_op(3, 1, 256, 512)
+        c_op(3, 1, 256, 512)
+        e_op(3, 0, 256, 512)
+        q_op(3, 0, 256)
+        st2(0, 3, 1)
+        pl(3, 3, 256, 512)
+        b_op(3, 2, 256, 512)
+        c_op(3, 2, 256, 512)
+        e_op(3, 1, 256, 512)
+        o_op(0, 3, 1, False)
+        b_op(3, 3, 256, 512)
+        c_op(3, 3, 256, 512)
+        e_op(3, 2, 256, 512)
+        e_op(3, 3, 256, 512)
+        for i in (0, 1):
+            for o in (0, 1):
+                st2(1, i, o)
+                o_op(1, i, o, True)
+        for i in (2, 3):
+            f_op(3, 128 * i, 128 * i + 128)
+            q_op(3, 128 * i, 128 * i + 128)
+            for o in (0, 1):
+                st2(1, i, o)
+        for i in (2, 3):
+            for o in (0, 1):
+                o_op(1, i, o, o == 1)

@@ -17,7 +17,8 @@ FP4X4 = mybir.dt.float4_e2m1fn_x4
 ADD = mybir.AluOpType.add
 MULT = mybir.AluOpType.mult
 COPY = mybir.ActivationFunctionType.Copy
-TANH = mybir.ActivationFunctionType.Tanh
+IDENTITY = mybir.ActivationFunctionType.Identity
+SIGMOID = mybir.ActivationFunctionType.Sigmoid
 
 P = 128
 
@@ -29,7 +30,7 @@ def tile_inversegainlatentresidualpredictionsynth_d1p_kernel(
     with ExitStack() as ctx:
         keep = ctx.enter_context(tc.tile_pool(name="keep", bufs=1))
         work = ctx.enter_context(tc.tile_pool(name="work", bufs=3))
-        psum = ctx.enter_context(tc.psum_pool(name="psum", bufs=8))
+        psum = ctx.enter_context(tc.psum_pool(name="psum", bufs=4))
         ctx.enter_context(tc.manual_schedule())
 
         ident = keep.tile([P, P], F32, name="ident")
@@ -54,19 +55,21 @@ def tile_inversegainlatentresidualpredictionsynth_d1p_kernel(
         cb_v = c_bytes.rearrange("(p i) k -> p i k", i=8)
         q_v = q.rearrange("(p i) c -> p i c", i=8)
         wq_v = wq.rearrange("(g p t) c -> g p t c", p=P, t=4)
-        nc.sync.dma_start(out=csc[:], in_=c_scale.rearrange("(p i) j -> p (i j)", i=8))
-        nc.sync.dma_start(out=c8[0][:], in_=cb_v[:, 0:4, :])
-        nc.sync.dma_start(out=qs[0][0][:], in_=q_v[:, 0:2, :])
-        nc.sync.dma_start(out=qs[0][1][:], in_=q_v[:, 2:4, :])
-        for qd in range(4):
-            rows = slice(32 * qd, 32 * qd + 4)
-            nc.scalar.dma_start(out=wl_sr[rows, :].bitcast(I32), in_=wl_scales[0, 4 * qd : 4 * qd + 4, :].bitcast(I32))
-            nc.gpsimd.dma_start(out=wm_sr[rows, :].bitcast(I32), in_=wm_scales[0, 4 * qd : 4 * qd + 4, :].bitcast(I32))
-        nc.sync.dma_start(out=igb[:], in_=ig.rearrange("(g p t) -> p g t", p=P, t=4))
+        for i in range(4):
+            nc.sync.dma_start(out=qs[0][i // 2][:, i % 2, :], in_=q_v[:, i, :])
         for gk in range(2):
             nc.sync.dma_start(out=wqs[0][:, gk, :, :], in_=wq_v[gk, :, :, 0:512])
+        nc.sync.dma_start(out=igb[:], in_=ig.rearrange("(g p t) -> p g t", p=P, t=4))
+        nc.sync.dma_start(out=csc[:], in_=c_scale.rearrange("(p i) j -> p (i j)", i=8))
+        nc.sync.dma_start(out=c8[0][:], in_=cb_v[:, 0:4, :])
+        for qd4 in range(4):
+            rows = slice(32 * qd4, 32 * qd4 + 4)
+            nc.sync.dma_start(out=wl_sr[rows, :].bitcast(I32), in_=wl_scales[0, 4 * qd4 : 4 * qd4 + 4, :].bitcast(I32))
         nc.sync.dma_start(out=wl_w[:].bitcast(I32), in_=wl_words[0].bitcast(I32))
         nc.sync.dma_start(out=wm_w[:].bitcast(I32), in_=wm_words[0].bitcast(I32))
+        for qd4 in range(4):
+            rows = slice(32 * qd4, 32 * qd4 + 4)
+            nc.sync.dma_start(out=wm_sr[rows, :].bitcast(I32), in_=wm_scales[0, 4 * qd4 : 4 * qd4 + 4, :].bitcast(I32))
         nc.sync.dma_start(out=c8[1][:], in_=cb_v[:, 4:8, :])
         for gk in range(2):
             nc.sync.dma_start(out=wqs[1][:, gk, :, :], in_=wq_v[gk, :, :, 512:1024])
@@ -82,10 +85,11 @@ def tile_inversegainlatentresidualpredictionsynth_d1p_kernel(
                 )
 
         warm = keep.tile([P, 1], F32, name="warm")
-        nc.scalar.activation(out=warm[:], in_=ident[:, 0:1], func=TANH)
+        nc.scalar.activation(out=warm[:], in_=ident[:, 0:1], func=SIGMOID)
         igf = keep.tile([P, 8], F32, name="igf")
         igh = keep.tile([P, 8], F32, name="igh")
 
+        qd = [keep.tile([P, 2, 512], I32, name="qd0"), keep.tile([P, 2, 512], I32, name="qd1")]
         qt = [keep.tile([P, 2, 2, 512], F32, name="qt0"), keep.tile([P, 2, 2, 512], F32, name="qt1")]
         cbf = keep.tile([P, 8, 512], BF16, name="cbf")
         cq = [keep.tile([P, 512], U32, name="cq0", align_bytes=64), keep.tile([P, 512], U32, name="cq1", align_bytes=64)]
@@ -97,8 +101,8 @@ def tile_inversegainlatentresidualpredictionsynth_d1p_kernel(
         yq = [keep.tile([P, 2, 512], U32, name="yq0", align_bytes=64), keep.tile([P, 2, 512], U32, name="yq1", align_bytes=64)]
         yqs = [keep.tile([P, 2, 512], U8, name="yqs0", align_bytes=64), keep.tile([P, 2, 512], U8, name="yqs1", align_bytes=64)]
 
-        def widen(h, i, on_scalar):
-            for j in range(4):
+        def widen(h, i, on_scalar, js=(0, 1, 2, 3)):
+            for j in js:
                 ks = slice(128 * j, 128 * j + 128)
                 src = c8[h][:, i, ks].bitcast(FP8)
                 col = csc[:, 4 * (4 * h + i) + j : 4 * (4 * h + i) + j + 1]
@@ -117,7 +121,7 @@ def tile_inversegainlatentresidualpredictionsynth_d1p_kernel(
         grp = {}
 
         def c_turn(h, pair, on_scalar):
-            bank = psum.tile([P, 2, 2, 128], F32, name="bank", tag="bank")
+            bank = psum.tile([P, 2, 2, 128], F32, name="bank", tag="bank", bufs=4)
             for j in range(2):
                 words = cbf[:, 4 * h + 2 * pair + j, :].bitcast(F32)
                 for u in range(2):
@@ -133,24 +137,39 @@ def tile_inversegainlatentresidualpredictionsynth_d1p_kernel(
                 out=cq[h][:].bitcast(FP8X4), scales=cqs[h][:], in_=grp[h][:].rearrange("p n t -> p (n t)")
             )
 
-        def q_turn(h, pair, g, on_scalar):
-            bank = psum.tile([P, 2, 2, 128], F32, name="bank", tag="bank")
+        def q_sort(pair):
             for j in range(2):
-                words = qs[h][pair][:, j, :].bitcast(F32)
-                for u in range(2):
-                    nc.tensor.transpose(bank[:, u, j, :], words[:, 256 * g + u : 256 * g + 256 : 2], ident[:])
-            copy(
-                on_scalar,
-                qt[h][:, g, :, 256 * pair : 256 * pair + 256],
-                bank[:].rearrange("p u j n -> p u (j n)"),
-            )
+                nc.gpsimd.tensor_copy(
+                    out=qd[pair][:, j, :].rearrange("p (g u w) -> p g u w", g=2, u=2),
+                    in_=qs[1][pair][:, j, :].bitcast(I32).rearrange("p (g w u) -> p g u w", g=2, u=2),
+                )
+
+        def q_turn(h, pair, first_on_scalar):
+            banks = []
+            for g in range(2):
+                bank = psum.tile([P, 2, 2, 128], F32, name="bank", tag="bank", bufs=4)
+                banks.append(bank)
+            for j in range(2):
+                for g in range(2):
+                    for u in range(2):
+                        if h == 0:
+                            words = qs[h][pair][:, j, :].bitcast(F32)[:, 256 * g + u : 256 * g + 256 : 2]
+                        else:
+                            words = qd[pair][:, j, :].bitcast(F32)[:, 256 * g + 128 * u : 256 * g + 128 * u + 128]
+                        nc.tensor.transpose(banks[g][:, u, j, :], words, ident[:])
+            for g in range(2):
+                copy(
+                    (g == 0) == first_on_scalar,
+                    qt[h][:, g, :, 256 * pair : 256 * pair + 256],
+                    banks[g][:].rearrange("p u j n -> p u (j n)"),
+                )
 
         def qt_view(h, g, t):
             return qt[h][:, g, t // 2, :].bitcast(BF16)[:, t % 2 : 1024 : 2]
 
-        def permute_words(g, eng):
+        def permute_words(g, eng, which):
             b = slice(1024 * g, 1024 * g + 1024)
-            for src, dst in ((wl_w, wl_p), (wm_w, wm_p)):
+            for src, dst in (((wl_w, wl_p), (wm_w, wm_p))[which],):
                 eng.tensor_copy(
                     out=dst[:, b].rearrange("p (t m b) -> p t m b", t=4, b=2),
                     in_=src[:, b].rearrange("p (m t b) -> p t m b", t=4, b=2),
@@ -169,7 +188,7 @@ def tile_inversegainlatentresidualpredictionsynth_d1p_kernel(
 
         def pl(u, t, n0=0, n1=512):
             h, g = units[u]
-            bank = psum.tile([P, n1 - n0], F32, name="bank", tag="bank")
+            bank = psum.tile([P, n1 - n0], F32, name="plain", tag="plain", bufs=4)
             st["pl", u, t, n0] = bank
             n = 0
             for gk in range(2):
@@ -186,7 +205,7 @@ def tile_inversegainlatentresidualpredictionsynth_d1p_kernel(
         def mx1(u, t, wp, wsp, key):
             h, g = units[u]
             k = 4 * g + t
-            bank = psum.tile([P, 512], F32, name="bank", tag="bank")
+            bank = psum.tile([P, 512], F32, name="bank", tag="bank", bufs=4)
             st[key, u, t] = bank
             nc.tensor.matmul_mx(
                 out=bank[:],
@@ -200,9 +219,12 @@ def tile_inversegainlatentresidualpredictionsynth_d1p_kernel(
 
         def igq(u, t):
             h, g = units[u]
-            z = work.tile([P, 512], F32, name="igqt", bufs=5)
+            z = work.tile([P, 512], F32, name="igqt", bufs=7)
             st["igq", u, t] = z
-            nc.scalar.activation(out=z[:], in_=qt_view(h, g, t), func=COPY, scale=igf[:, 4 * g + t : 4 * g + t + 1])
+            nc.scalar.activation(
+                out=z[:], in_=qt_view(h, g, t), func=IDENTITY,
+                scale=igf[:, 4 * g + t : 4 * g + t + 1], bias=igh[:, 4 * g + t : 4 * g + t + 1],
+            )
 
         def mx_pair(u, t):
             mx1(u, t, wl_p, wl_sp, "mxl")
@@ -214,13 +236,18 @@ def tile_inversegainlatentresidualpredictionsynth_d1p_kernel(
             nc.scalar.copy(out=z[:], in_=st["mxl", u, t][:])
 
         def d_op(u, t):
-            g = units[u][1]
-            z = work.tile([P, 512], F32, name="wsum", bufs=5)
+            h, g = units[u]
+            z = work.tile([P, 512], F32, name="wsum", bufs=7)
             st["w", u, t] = z
-            nc.vector.scalar_tensor_tensor(
-                out=z[:], in0=st["mxm", u, t][:], scalar=igf[:, 4 * g + t : 4 * g + t + 1], in1=st["igq", u, t][:],
-                op0=MULT, op1=ADD,
-            )
+            if u == 3:
+                nc.vector.scalar_tensor_tensor(
+                    out=z[:], in0=st["mxm", u, t][:], scalar=igf[:, 4 * g + t : 4 * g + t + 1], in1=st["igq", u, t][:],
+                    op0=MULT, op1=ADD,
+                )
+            else:
+                nc.vector.scalar_tensor_tensor(
+                    out=z[:], in0=st["mxm", u, t][:], scalar=-0.5, in1=qt_view(h, g, t), op0=ADD, op1=ADD,
+                )
 
         def b_op(u, t, n0=0, n1=512):
             z = work.tile([P, n1 - n0], F32, name="lsum", bufs=3)
@@ -228,18 +255,32 @@ def tile_inversegainlatentresidualpredictionsynth_d1p_kernel(
             nc.vector.tensor_tensor(out=z[:], in0=st["pl", u, t, n0][:], in1=st["lmx", u, t][:, n0:n1], op=ADD)
 
         def c_op(u, t, n0=0, n1=512):
-            z = work.tile([P, n1 - n0], F32, name="th", bufs=3)
+            z = work.tile([P, n1 - n0], F32, name="th", bufs=5)
             st["th", u, t, n0] = z
-            nc.scalar.activation(out=z[:], in_=st["ls", u, t, n0][:], func=TANH)
+            nc.scalar.activation(out=z[:], in_=st["ls", u, t, n0][:], func=SIGMOID, scale=2.0)
 
         def e_op(u, t, n0=0, n1=512):
             g = units[u][1]
-            if t == 0 and n0 == 0:
+            if u == 3:
+                if t == 0 and n0 == 0:
+                    ye = work.tile([P, 4, 512], BF16, name="ye", bufs=2)
+                    st["ye", u] = ye
+                nc.vector.scalar_tensor_tensor(
+                    out=st["ye", u][:, t, n0:n1], in0=st["th", u, t, n0][:], scalar=igf[:, 4 * g + t : 4 * g + t + 1],
+                    in1=st["w", u, t][:, n0:n1], op0=MULT, op1=ADD,
+                )
+            else:
+                z = work.tile([P, 512], F32, name="ysum", bufs=6)
+                st["y", u, t] = z
+                nc.gpsimd.tensor_tensor(out=z[:], in0=st["th", u, t, 0][:], in1=st["w", u, t][:], op=ADD)
+
+        def x_op(u, t):
+            g = units[u][1]
+            if t == 0:
                 ye = work.tile([P, 4, 512], BF16, name="ye", bufs=2)
                 st["ye", u] = ye
-            nc.vector.scalar_tensor_tensor(
-                out=st["ye", u][:, t, n0:n1], in0=st["th", u, t, n0][:], scalar=igh[:, 4 * g + t : 4 * g + t + 1],
-                in1=st["w", u, t][:, n0:n1], op0=MULT, op1=ADD,
+            nc.scalar.activation(
+                out=st["ye", u][:, t, :], in_=st["y", u, t][:], func=COPY, scale=igf[:, 4 * g + t : 4 * g + t + 1]
             )
 
         def f_op(u, n0, n1):
@@ -261,7 +302,7 @@ def tile_inversegainlatentresidualpredictionsynth_d1p_kernel(
         out_v = out.rearrange("(p i) o -> p i o", i=8)
 
         def st2(h, i, o):
-            bank = psum.tile([P, 512], F32, name="bank", tag="bank")
+            bank = psum.tile([P, 512], F32, name="bank", tag="bank", bufs=4)
             st["o", h, i, o] = bank
             for g in range(2):
                 nc.tensor.matmul_mx(
@@ -279,125 +320,100 @@ def tile_inversegainlatentresidualpredictionsynth_d1p_kernel(
             copy(on_scalar, ot[:], st["o", h, i, o][:])
             nc.sync.dma_start(out=out_v[:, 4 * h + i, 512 * o : 512 * o + 512], in_=ot[:])
 
+        q_turn(0, 0, False)
+        q_turn(0, 1, False)
+        pl(0, 0)
         widen(0, 0, False)
-        widen(0, 1, True)
-        widen(0, 2, False)
+        widen(0, 1, False)
         widen(0, 3, True)
-        c_turn(0, 0, False)
-        c_turn(0, 1, True)
-        q_turn(0, 0, 0, False)
-        q_turn(0, 0, 1, True)
-        c_quant(0)
-        q_turn(0, 1, 0, False)
-        q_turn(0, 1, 1, True)
+        widen(0, 2, False, (0, 1))
+        widen(0, 2, True, (2, 3))
+        pl(0, 1)
+        permute_words(0, nc.vector, 0)
         nc.vector.tensor_copy(out=igf[:], in_=igb[:])
-        nc.vector.tensor_scalar(out=igh[:], in0=igb[:], scalar1=0.5, scalar2=None, op0=MULT)
-        for t in range(4):
-            igq(0, t)
+        nc.vector.tensor_scalar(out=igh[:], in0=igb[:], scalar1=-0.5, scalar2=None, op0=MULT)
         permute_scales(0)
         permute_scales(1)
-        permute_words(0, nc.vector)
-        permute_words(1, nc.gpsimd)
-        for i in range(4):
-            widen(1, i, i % 2 == 1)
-        pl(0, 0)
-        pl(0, 1)
-        mx_pair(0, 0)
-        a_op(0, 0)
-        d_op(0, 0)
-        mx_pair(0, 1)
-        a_op(0, 1)
-        b_op(0, 0)
-        c_op(0, 0)
-        d_op(0, 1)
-        b_op(0, 1)
-        c_op(0, 1)
-        e_op(0, 0)
+        c_turn(0, 0, False)
+        c_turn(0, 1, True)
+        permute_words(0, nc.vector, 1)
+        c_quant(0)
+        permute_words(1, nc.gpsimd, 0)
+        permute_words(1, nc.gpsimd, 1)
+        q_sort(0)
+        q_sort(1)
+        widen(1, 0, False)
         pl(0, 2)
-        mx_pair(0, 2)
-        a_op(0, 2)
-        e_op(0, 1)
-        b_op(0, 2)
-        d_op(0, 2)
-        c_op(0, 2)
-        igq(1, 0)
-        pl(0, 3)
-        mx_pair(0, 3)
-        a_op(0, 3)
-        e_op(0, 2)
-        b_op(0, 3)
-        d_op(0, 3)
-        c_op(0, 3)
-        slots = [(u, t) for u in (1, 2) for t in range(4)]
+        seq = [(u, t) for u in range(3) for t in range(4)] + [(3, 0), (3, 1), (3, 2), (3, 3)]
         extra = {
-            (1, 0): [lambda: c_turn(1, 0, False), lambda: c_turn(1, 1, True)],
-            (1, 1): [lambda: q_turn(1, 0, 0, False), lambda: q_turn(1, 0, 1, True)],
-            (1, 2): [lambda: c_quant(1), lambda: q_turn(1, 1, 0, False), lambda: q_turn(1, 1, 1, True)],
+            (1, 1): [lambda: c_turn(1, 0, False), lambda: c_turn(1, 1, True)],
+            (1, 2): [lambda: c_quant(1), lambda: q_turn(1, 0, False)],
+            (1, 3): [lambda: q_turn(1, 1, False)],
+            (1, 0): [],
         }
-        plan = {(2, 2): [(0, 0), (0, 1)], (2, 3): [(1, 0), (1, 1), (2, 0)]}
-        for s, (u, t) in enumerate(slots):
-            pu, pt = (u, t - 1) if t else (u - 1, 3)
+        late = {
+            (2, 0): [lambda: f_op(0, 0, 512), lambda: q_op(0, 0, 512)],
+            (2, 2): [lambda: f_op(1, 0, 512), lambda: q_op(1, 0, 512)],
+            (3, 2): [lambda: f_op(2, 0, 256)],
+            (3, 3): [lambda: f_op(2, 256, 512), lambda: q_op(2, 0, 512)],
+        }
+        x_at = {5: [0], 6: [1, 2], 7: [3, 4], 8: [5, 6], 9: [7], 10: [8], 11: [9], 12: [10], 13: [11]}
+        for s, (u, t) in enumerate(seq):
+            if s == 2:
+                pl(0, 3)
             mx_pair(u, t)
             a_op(u, t)
-            if s:
-                b_op(pu, pt)
-                c_op(pu, pt)
-            d_op(u, t)
-            e_op(pu, pt)
+            if u == 3:
+                st2(0, t // 2, t % 2)
             for f in extra.get((u, t), []):
                 f()
-            for i, o in plan.get((u, t), []):
-                st2(0, i, o)
-            pl(u, t)
-            igq(*((u, t + 1) if t < 3 else (u + 1, 0)))
-            for i, o in plan.get((u, t), []):
-                o_op(0, i, o, True)
-            if t == 0:
-                f_op(u - 1, 0, 512)
-                q_op(u - 1, 0, 512)
-        for t in range(4):
-            mx_pair(3, t)
-            a_op(3, t)
-            if t == 0:
-                b_op(2, 3)
-                c_op(2, 3)
-            else:
-                b_op(3, t - 1, 0, 256)
-                c_op(3, t - 1, 0, 256)
-            d_op(3, t)
-            if t == 0:
-                e_op(2, 3)
-            else:
-                e_op(3, t - 1, 0, 256)
-            if t < 3:
-                igq(3, t + 1)
-            if t == 1:
-                f_op(2, 0, 512)
-                q_op(2, 0, 512)
-            pl(3, t, 0, 256)
+            if u == 3:
+                pl(3, t, 0, 256)
+            elif u:
+                pl(u, t)
+            if s:
+                pu, pt = seq[s - 1]
+                n1 = 256 if pu == 3 else 512
+                b_op(pu, pt, 0, n1)
+                c_op(pu, pt, 0, n1)
+            d_op(u, t)
+            if s:
+                e_op(pu, pt, 0, n1)
+            for k in x_at.get(s, []):
+                x_op(*seq[k])
+            if u == 0 and t:
+                widen(1, t, False)
+            if u == 2:
+                igq(3, t)
+            if u == 3:
+                o_op(0, t // 2, t % 2, True)
+            for f in late.get((u, t), []):
+                f()
         pl(3, 0, 256, 512)
         b_op(3, 3, 0, 256)
         c_op(3, 3, 0, 256)
-        st2(0, 2, 1)
-        o_op(0, 2, 1, True)
+        st2(0, 2, 0)
+        o_op(0, 2, 0, True)
         pl(3, 1, 256, 512)
         b_op(3, 0, 256, 512)
         e_op(3, 3, 0, 256)
         c_op(3, 0, 256, 512)
         f_op(3, 0, 256)
-        st2(0, 3, 0)
-        o_op(0, 3, 0, True)
+        st2(0, 2, 1)
+        o_op(0, 2, 1, True)
         pl(3, 2, 256, 512)
         b_op(3, 1, 256, 512)
         c_op(3, 1, 256, 512)
         e_op(3, 0, 256, 512)
         q_op(3, 0, 256)
-        st2(0, 3, 1)
+        st2(0, 3, 0)
         pl(3, 3, 256, 512)
         b_op(3, 2, 256, 512)
         c_op(3, 2, 256, 512)
         e_op(3, 1, 256, 512)
-        o_op(0, 3, 1, False)
+        o_op(0, 3, 0, False)
+        st2(0, 3, 1)
+        o_op(0, 3, 1, True)
         b_op(3, 3, 256, 512)
         c_op(3, 3, 256, 512)
         e_op(3, 2, 256, 512)

@@ -55,21 +55,21 @@ def tile_inversegainlatentresidualpredictionsynth_d1p_kernel(
         cb_v = c_bytes.rearrange("(p i) k -> p i k", i=8)
         q_v = q.rearrange("(p i) c -> p i c", i=8)
         wq_v = wq.rearrange("(g p t) c -> g p t c", p=P, t=4)
-        for i in range(4):
-            nc.sync.dma_start(out=qs[0][i // 2][:, i % 2, :], in_=q_v[:, i, :])
+        for i in range(2):
+            nc.sync.dma_start(out=qs[0][0][:, i, :], in_=q_v[:, i, :])
+        for qd4 in range(4):
+            rows = slice(32 * qd4, 32 * qd4 + 4)
+            nc.scalar.dma_start(out=wl_sr[rows, :].bitcast(I32), in_=wl_scales[0, 4 * qd4 : 4 * qd4 + 4, :].bitcast(I32))
+            nc.gpsimd.dma_start(out=wm_sr[rows, :].bitcast(I32), in_=wm_scales[0, 4 * qd4 : 4 * qd4 + 4, :].bitcast(I32))
+        for i in range(2):
+            nc.sync.dma_start(out=qs[0][1][:, i, :], in_=q_v[:, 2 + i, :])
         for gk in range(2):
             nc.sync.dma_start(out=wqs[0][:, gk, :, :], in_=wq_v[gk, :, :, 0:512])
-        nc.sync.dma_start(out=igb[:], in_=ig.rearrange("(g p t) -> p g t", p=P, t=4))
         nc.sync.dma_start(out=csc[:], in_=c_scale.rearrange("(p i) j -> p (i j)", i=8))
         nc.sync.dma_start(out=c8[0][:], in_=cb_v[:, 0:4, :])
-        for qd4 in range(4):
-            rows = slice(32 * qd4, 32 * qd4 + 4)
-            nc.sync.dma_start(out=wl_sr[rows, :].bitcast(I32), in_=wl_scales[0, 4 * qd4 : 4 * qd4 + 4, :].bitcast(I32))
         nc.sync.dma_start(out=wl_w[:].bitcast(I32), in_=wl_words[0].bitcast(I32))
+        nc.sync.dma_start(out=igb[:], in_=ig.rearrange("(g p t) -> p g t", p=P, t=4))
         nc.sync.dma_start(out=wm_w[:].bitcast(I32), in_=wm_words[0].bitcast(I32))
-        for qd4 in range(4):
-            rows = slice(32 * qd4, 32 * qd4 + 4)
-            nc.sync.dma_start(out=wm_sr[rows, :].bitcast(I32), in_=wm_scales[0, 4 * qd4 : 4 * qd4 + 4, :].bitcast(I32))
         nc.sync.dma_start(out=c8[1][:], in_=cb_v[:, 4:8, :])
         for gk in range(2):
             nc.sync.dma_start(out=wqs[1][:, gk, :, :], in_=wq_v[gk, :, :, 512:1024])
@@ -139,7 +139,7 @@ def tile_inversegainlatentresidualpredictionsynth_d1p_kernel(
 
         def q_sort(pair):
             for j in range(2):
-                nc.gpsimd.tensor_copy(
+                nc.vector.tensor_copy(
                     out=qd[pair][:, j, :].rearrange("p (g u w) -> p g u w", g=2, u=2),
                     in_=qs[1][pair][:, j, :].bitcast(I32).rearrange("p (g w u) -> p g u w", g=2, u=2),
                 )
@@ -175,10 +175,10 @@ def tile_inversegainlatentresidualpredictionsynth_d1p_kernel(
                     in_=src[:, b].rearrange("p (m t b) -> p t m b", t=4, b=2),
                 )
 
-        def permute_scales(g):
+        def permute_scales(g, eng, which):
             b = slice(512 * g, 512 * g + 512)
-            for src, dst in ((wl_sr, wl_sp), (wm_sr, wm_sp)):
-                nc.gpsimd.tensor_copy(
+            for src, dst in (((wl_sr, wl_sp), (wm_sr, wm_sp))[which],):
+                eng.tensor_copy(
                     out=dst[:, b].rearrange("p (t m) -> p t m", t=4),
                     in_=src[:, b].rearrange("p (m t) -> p t m", t=4),
                 )
@@ -323,6 +323,7 @@ def tile_inversegainlatentresidualpredictionsynth_d1p_kernel(
         q_turn(0, 0, False)
         q_turn(0, 1, False)
         pl(0, 0)
+        permute_scales(0, nc.vector, 0)
         widen(0, 0, False)
         widen(0, 1, False)
         widen(0, 3, True)
@@ -332,16 +333,14 @@ def tile_inversegainlatentresidualpredictionsynth_d1p_kernel(
         permute_words(0, nc.vector, 0)
         nc.vector.tensor_copy(out=igf[:], in_=igb[:])
         nc.vector.tensor_scalar(out=igh[:], in0=igb[:], scalar1=-0.5, scalar2=None, op0=MULT)
-        permute_scales(0)
-        permute_scales(1)
+        permute_scales(1, nc.gpsimd, 0)
+        permute_scales(1, nc.gpsimd, 1)
+        permute_words(1, nc.gpsimd, 1)
+        permute_words(0, nc.vector, 1)
         c_turn(0, 0, False)
         c_turn(0, 1, True)
-        permute_words(0, nc.vector, 1)
         c_quant(0)
-        permute_words(1, nc.gpsimd, 0)
-        permute_words(1, nc.gpsimd, 1)
-        q_sort(0)
-        q_sort(1)
+        permute_scales(0, nc.vector, 1)
         widen(1, 0, False)
         pl(0, 2)
         seq = [(u, t) for u in range(3) for t in range(4)] + [(3, 0), (3, 1), (3, 2), (3, 3)]
@@ -381,8 +380,17 @@ def tile_inversegainlatentresidualpredictionsynth_d1p_kernel(
                 e_op(pu, pt, 0, n1)
             for k in x_at.get(s, []):
                 x_op(*seq[k])
-            if u == 0 and t:
-                widen(1, t, False)
+            if s == 1:
+                permute_words(1, nc.vector, 0)
+                widen(1, 1, True)
+            if s == 2:
+                widen(1, 2, False)
+            if s == 3:
+                widen(1, 3, False)
+            if s == 4:
+                q_sort(0)
+            if s == 5:
+                q_sort(1)
             if u == 2:
                 igq(3, t)
             if u == 3:

@@ -48,6 +48,8 @@ def tile_inversegainlatentresidualpredictionsynth_d1p_kernel(
         ws_w = keep.tile([P, 2, 2048], U8, name="ws_w", align_bytes=64)
         ws_s = keep.tile([P, 2, 1024], U8, name="ws_s", align_bytes=64)
 
+        zero = keep.tile([P, 512], BF16, name="zero")
+        nc.vector.memset(zero[:], 0.0)
         nc.vector.memset(wl_sr[:].bitcast(I32), 0)
         nc.vector.memset(wm_sr[:].bitcast(I32), 0)
         nc.vector.memset(ws_s[:].rearrange("p g n -> p (g n)").bitcast(I32), 0)
@@ -121,7 +123,7 @@ def tile_inversegainlatentresidualpredictionsynth_d1p_kernel(
         grp = {}
 
         def c_turn(h, pair, on_scalar):
-            bank = psum.tile([P, 2, 2, 128], F32, name="bank", tag="bank", bufs=4)
+            bank = psum.tile([P, 2, 2, 128], F32, name="bank", tag=("bank", "plain")[h], bufs=4)
             for j in range(2):
                 words = cbf[:, 4 * h + 2 * pair + j, :].bitcast(F32)
                 for u in range(2):
@@ -147,7 +149,7 @@ def tile_inversegainlatentresidualpredictionsynth_d1p_kernel(
         def q_turn(h, pair, first_on_scalar):
             banks = []
             for g in range(2):
-                bank = psum.tile([P, 2, 2, 128], F32, name="bank", tag="bank", bufs=4)
+                bank = psum.tile([P, 2, 2, 128], F32, name="bank", tag=("bank", "plain")[h], bufs=4)
                 banks.append(bank)
             for j in range(2):
                 for g in range(2):
@@ -186,21 +188,26 @@ def tile_inversegainlatentresidualpredictionsynth_d1p_kernel(
         units = [(0, 0), (0, 1), (1, 0), (1, 1)]
         st = {}
 
-        def pl(u, t, n0=0, n1=512):
+        def pl(u, t, n0=0, n1=512, between=()):
             h, g = units[u]
             bank = psum.tile([P, n1 - n0], F32, name="plain", tag="plain", bufs=4)
             st["pl", u, t, n0] = bank
-            n = 0
             for gk in range(2):
                 for tk in range(4):
                     nc.tensor.matmul(
                         bank[:],
                         lhsT=wqs[g][:, gk, tk, t : 512 : 4],
                         rhs=qt_view(h, gk, tk)[:, n0:n1],
-                        start=(n == 0),
-                        stop=(n == 7),
+                        start=(gk == 0 and tk == 0),
+                        stop=(gk == 1 and tk == 3),
                     )
-                    n += 1
+                if gk == 0:
+                    for f in between:
+                        f()
+
+        def keep_warm(count):
+            for k in range(count):
+                nc.tensor.matmul(warm_bank[:], lhsT=zero[:, 0:128], rhs=zero[:], start=True, stop=True)
 
         def mx1(u, t, wp, wsp, key):
             h, g = units[u]
@@ -320,8 +327,12 @@ def tile_inversegainlatentresidualpredictionsynth_d1p_kernel(
             copy(on_scalar, ot[:], st["o", h, i, o][:])
             nc.sync.dma_start(out=out_v[:, 4 * h + i, 512 * o : 512 * o + 512], in_=ot[:])
 
+        warm_bank = psum.tile([P, 512], F32, name="warm_bank", tag="plain", bufs=4)
+        keep_warm(5)
         q_turn(0, 0, False)
+        keep_warm(2)
         q_turn(0, 1, False)
+        keep_warm(2)
         pl(0, 0)
         permute_scales(0, nc.vector, 0)
         widen(0, 0, False)
@@ -364,12 +375,10 @@ def tile_inversegainlatentresidualpredictionsynth_d1p_kernel(
             a_op(u, t)
             if u == 3:
                 st2(0, t // 2, t % 2)
-            for f in extra.get((u, t), []):
-                f()
             if u == 3:
                 pl(3, t, 0, 256)
             elif u:
-                pl(u, t)
+                pl(u, t, 0, 512, extra.get((u, t), []))
             if s:
                 pu, pt = seq[s - 1]
                 n1 = 256 if pu == 3 else 512

@@ -61,12 +61,14 @@ def tile_inversegainlatentresidualpredictionsynth_d1p_kernel(
             nc.sync.dma_start(out=qs[0][0][:, i, :], in_=q_v[:, i, :])
         for qd4 in range(4):
             rows = slice(32 * qd4, 32 * qd4 + 4)
-            nc.scalar.dma_start(out=wl_sr[rows, :].bitcast(I32), in_=wl_scales[0, 4 * qd4 : 4 * qd4 + 4, :].bitcast(I32))
             nc.gpsimd.dma_start(out=wm_sr[rows, :].bitcast(I32), in_=wm_scales[0, 4 * qd4 : 4 * qd4 + 4, :].bitcast(I32))
         for i in range(2):
             nc.sync.dma_start(out=qs[0][1][:, i, :], in_=q_v[:, 2 + i, :])
-        for gk in range(2):
-            nc.sync.dma_start(out=wqs[0][:, gk, :, :], in_=wq_v[gk, :, :, 0:512])
+        nc.sync.dma_start(out=wqs[0][:, 0, :, :], in_=wq_v[0, :, :, 0:512])
+        for qd4 in range(4):
+            rows = slice(32 * qd4, 32 * qd4 + 4)
+            nc.scalar.dma_start(out=wl_sr[rows, :].bitcast(I32), in_=wl_scales[0, 4 * qd4 : 4 * qd4 + 4, :].bitcast(I32))
+        nc.sync.dma_start(out=wqs[0][:, 1, :, :], in_=wq_v[1, :, :, 0:512])
         nc.sync.dma_start(out=csc[:], in_=c_scale.rearrange("(p i) j -> p (i j)", i=8))
         nc.sync.dma_start(out=c8[0][:], in_=cb_v[:, 0:4, :])
         nc.sync.dma_start(out=wl_w[:].bitcast(I32), in_=wl_words[0].bitcast(I32))
@@ -332,7 +334,7 @@ def tile_inversegainlatentresidualpredictionsynth_d1p_kernel(
         q_turn(0, 0, False)
         keep_warm(2)
         q_turn(0, 1, False)
-        keep_warm(2)
+        keep_warm(1)
         pl(0, 0)
         permute_scales(0, nc.vector, 0)
         widen(0, 0, False)
@@ -344,10 +346,9 @@ def tile_inversegainlatentresidualpredictionsynth_d1p_kernel(
         permute_words(0, nc.vector, 0)
         nc.vector.tensor_copy(out=igf[:], in_=igb[:])
         nc.vector.tensor_scalar(out=igh[:], in0=igb[:], scalar1=-0.5, scalar2=None, op0=MULT)
+        permute_words(0, nc.gpsimd, 1)
         permute_scales(1, nc.gpsimd, 0)
         permute_scales(1, nc.gpsimd, 1)
-        permute_words(1, nc.gpsimd, 1)
-        permute_words(0, nc.vector, 1)
         c_turn(0, 0, False)
         c_turn(0, 1, True)
         c_quant(0)
@@ -371,13 +372,15 @@ def tile_inversegainlatentresidualpredictionsynth_d1p_kernel(
         for s, (u, t) in enumerate(seq):
             if s == 2:
                 pl(0, 3)
+            if s == 4:
+                pl(u, t)
             mx_pair(u, t)
             a_op(u, t)
             if u == 3:
                 st2(0, t // 2, t % 2)
             if u == 3:
                 pl(3, t, 0, 256)
-            elif u:
+            elif s > 4:
                 pl(u, t, 0, 512, extra.get((u, t), []))
             if s:
                 pu, pt = seq[s - 1]
@@ -393,8 +396,9 @@ def tile_inversegainlatentresidualpredictionsynth_d1p_kernel(
                 permute_words(1, nc.vector, 0)
                 widen(1, 1, True)
             if s == 2:
-                widen(1, 2, False)
+                permute_words(1, nc.vector, 1)
             if s == 3:
+                widen(1, 2, True)
                 widen(1, 3, False)
             if s == 4:
                 q_sort(0)
@@ -403,7 +407,7 @@ def tile_inversegainlatentresidualpredictionsynth_d1p_kernel(
             if u == 2:
                 igq(3, t)
             if u == 3:
-                o_op(0, t // 2, t % 2, True)
+                o_op(0, t // 2, t % 2, t % 2 == 1)
             for f in late.get((u, t), []):
                 f()
         pl(3, 0, 256, 512)

from contextlib import ExitStack

import concourse.mybir as mybir
from concourse.masks import make_identity

T, H, C, O = 1024, 512, 1024, 1024
FLOPS = 2 * T * H * C * 2 + 2 * T * C * C + 2 * T * C * O

F32 = mybir.dt.float32
BF16 = mybir.dt.bfloat16
I32 = mybir.dt.int32
U32 = mybir.dt.uint32
U8 = mybir.dt.uint8
FP8 = mybir.dt.float8_e4m3fn
FP8X4 = mybir.dt.float8_e4m3fn_x4
FP4X4 = mybir.dt.float4_e2m1fn_x4
ADD = mybir.AluOpType.add
MULT = mybir.AluOpType.mult
COPY = mybir.ActivationFunctionType.Copy
IDENTITY = mybir.ActivationFunctionType.Identity
SIGMOID = mybir.ActivationFunctionType.Sigmoid

P = 128


def tile_inversegainlatentresidualpredictionsynth_d1p_kernel(
    tc, c_bytes, c_scale, q, wm_words, wm_scales, wl_words, wl_scales, wq, ig, ws_words, ws_scales, out
):
    nc = tc.nc
    with ExitStack() as ctx:
        keep = ctx.enter_context(tc.tile_pool(name="keep", bufs=1))
        work = ctx.enter_context(tc.tile_pool(name="work", bufs=3))
        psum = ctx.enter_context(tc.psum_pool(name="psum", bufs=4))
        ctx.enter_context(tc.manual_schedule())

        ident = keep.tile([P, P], F32, name="ident")
        make_identity(nc, ident[:])
        c8 = [keep.tile([P, 4, 512], U8, name="c8_0"), keep.tile([P, 4, 512], U8, name="c8_1")]
        csc = keep.tile([P, 32], F32, name="csc")
        igb = keep.tile([P, 8], BF16, name="igb")
        qs = [[keep.tile([P, 2, 1024], BF16, name="qs00"), keep.tile([P, 2, 1024], BF16, name="qs01")],
              [keep.tile([P, 2, 1024], BF16, name="qs10"), keep.tile([P, 2, 1024], BF16, name="qs11")]]
        wqs = [keep.tile([P, 2, 4, 512], BF16, name="wqs0"), keep.tile([P, 2, 4, 512], BF16, name="wqs1")]
        wl_w = keep.tile([P, 2048], U8, name="wl_w")
        wm_w = keep.tile([P, 2048], U8, name="wm_w")
        wl_sr = keep.tile([P, 1024], U8, name="wl_sr")
        wm_sr = keep.tile([P, 1024], U8, name="wm_sr")
        ws_w = keep.tile([P, 2, 2048], U8, name="ws_w", align_bytes=64)
        ws_s = keep.tile([P, 2, 1024], U8, name="ws_s", align_bytes=64)

        zero = keep.tile([P, 512], BF16, name="zero")
        nc.vector.memset(zero[:], 0.0)
        nc.vector.memset(wl_sr[:].bitcast(I32), 0)
        nc.vector.memset(wm_sr[:].bitcast(I32), 0)
        nc.vector.memset(ws_s[:].rearrange("p g n -> p (g n)").bitcast(I32), 0)

        cb_v = c_bytes.rearrange("(p i) k -> p i k", i=8)
        q_v = q.rearrange("(p i) c -> p i c", i=8)
        wq_v = wq.rearrange("(g p t) c -> g p t c", p=P, t=4)
        for i in range(2):
            nc.sync.dma_start(out=qs[0][0][:, i, :], in_=q_v[:, i, :])
        for qd4 in range(4):
            rows = slice(32 * qd4, 32 * qd4 + 4)
            nc.gpsimd.dma_start(out=wm_sr[rows, :].bitcast(I32), in_=wm_scales[0, 4 * qd4 : 4 * qd4 + 4, :].bitcast(I32))
        for i in range(2):
            nc.sync.dma_start(out=qs[0][1][:, i, :], in_=q_v[:, 2 + i, :])
        nc.sync.dma_start(out=wqs[0][:, 0, :, :], in_=wq_v[0, :, :, 0:512])
        for qd4 in range(4):
            rows = slice(32 * qd4, 32 * qd4 + 4)
            nc.scalar.dma_start(out=wl_sr[rows, :].bitcast(I32), in_=wl_scales[0, 4 * qd4 : 4 * qd4 + 4, :].bitcast(I32))
        nc.sync.dma_start(out=wqs[0][:, 1, :, :], in_=wq_v[1, :, :, 0:512])
        nc.sync.dma_start(out=csc[:], in_=c_scale.rearrange("(p i) j -> p (i j)", i=8))
        nc.sync.dma_start(out=c8[0][:], in_=cb_v[:, 0:4, :])
        nc.sync.dma_start(out=wl_w[:].bitcast(I32), in_=wl_words[0].bitcast(I32))
        nc.sync.dma_start(out=igb[:], in_=ig.rearrange("(g p t) -> p g t", p=P, t=4))
        nc.sync.dma_start(out=wm_w[:].bitcast(I32), in_=wm_words[0].bitcast(I32))
        nc.sync.dma_start(out=c8[1][:], in_=cb_v[:, 4:8, :])
        for gk in range(2):
            nc.sync.dma_start(out=wqs[1][:, gk, :, :], in_=wq_v[gk, :, :, 512:1024])
        nc.sync.dma_start(out=qs[1][0][:], in_=q_v[:, 4:6, :])
        nc.sync.dma_start(out=qs[1][1][:], in_=q_v[:, 6:8, :])
        for g in range(2):
            nc.sync.dma_start(out=ws_w[:, g, :].bitcast(I32), in_=ws_words[g].bitcast(I32))
        for qd in range(4):
            for g in range(2):
                nc.sync.dma_start(
                    out=ws_s[32 * qd : 32 * qd + 4, g, :].bitcast(I32),
                    in_=ws_scales[g, 4 * qd : 4 * qd + 4, :].bitcast(I32),
                )

        warm = keep.tile([P, 1], F32, name="warm")
        nc.scalar.activation(out=warm[:], in_=ident[:, 0:1], func=SIGMOID)
        igf = keep.tile([P, 8], F32, name="igf")
        igh = keep.tile([P, 8], F32, name="igh")

        qd = [keep.tile([P, 2, 512], I32, name="qd0"), keep.tile([P, 2, 512], I32, name="qd1")]
        qt = [keep.tile([P, 2, 2, 512], F32, name="qt0"), keep.tile([P, 2, 2, 512], F32, name="qt1")]
        cbf = keep.tile([P, 8, 512], BF16, name="cbf")
        cq = [keep.tile([P, 512], U32, name="cq0", align_bytes=64), keep.tile([P, 512], U32, name="cq1", align_bytes=64)]
        cqs = [keep.tile([P, 512], U8, name="cqs0", align_bytes=64), keep.tile([P, 512], U8, name="cqs1", align_bytes=64)]
        wl_p = keep.tile([P, 2048], U8, name="wl_p", align_bytes=64)
        wm_p = keep.tile([P, 2048], U8, name="wm_p", align_bytes=64)
        wl_sp = keep.tile([P, 1024], U8, name="wl_sp", align_bytes=64)
        wm_sp = keep.tile([P, 1024], U8, name="wm_sp", align_bytes=64)
        yq = [keep.tile([P, 2, 512], U32, name="yq0", align_bytes=64), keep.tile([P, 2, 512], U32, name="yq1", align_bytes=64)]
        yqs = [keep.tile([P, 2, 512], U8, name="yqs0", align_bytes=64), keep.tile([P, 2, 512], U8, name="yqs1", align_bytes=64)]

        def widen(h, i, on_scalar, js=(0, 1, 2, 3)):
            for j in js:
                ks = slice(128 * j, 128 * j + 128)
                src = c8[h][:, i, ks].bitcast(FP8)
                col = csc[:, 4 * (4 * h + i) + j : 4 * (4 * h + i) + j + 1]
                dst = cbf[:, 4 * h + i, ks]
                if on_scalar:
                    nc.scalar.activation(out=dst, in_=src, func=COPY, scale=col)
                else:
                    nc.vector.tensor_scalar(out=dst, in0=src, scalar1=col, scalar2=None, op0=MULT)

        def copy(on_scalar, dst, src):
            if on_scalar:
                nc.scalar.copy(out=dst, in_=src)
            else:
                nc.vector.tensor_copy(out=dst, in_=src)

        grp = {}

        def c_turn(h, pair, on_scalar):
            bank = psum.tile([P, 2, 2, 128], F32, name="bank", tag=("bank", "plain")[h], bufs=4)
            for j in range(2):
                words = cbf[:, 4 * h + 2 * pair + j, :].bitcast(F32)
                for u in range(2):
                    nc.tensor.transpose(bank[:, u, j, :], words[:, u : 256 : 2], ident[:])
            if pair == 0:
                grouped = work.tile([P, 512, 4], BF16, name="grouped", align_bytes=64)
                grp[h] = grouped
            dst = grp[h][:].rearrange("p n t -> p (n t)").bitcast(F32).rearrange("p (n u) -> p n u", u=2)
            copy(on_scalar, dst[:, 256 * pair : 256 * pair + 256, :], bank[:].rearrange("p u j n -> p (j n) u"))

        def c_quant(h):
            nc.vector.quantize_mx(
                out=cq[h][:].bitcast(FP8X4), scales=cqs[h][:], in_=grp[h][:].rearrange("p n t -> p (n t)")
            )

        def q_sort(pair):
            for j in range(2):
                nc.vector.tensor_copy(
                    out=qd[pair][:, j, :].rearrange("p (g u w) -> p g u w", g=2, u=2),
                    in_=qs[1][pair][:, j, :].bitcast(I32).rearrange("p (g w u) -> p g u w", g=2, u=2),
                )

        def q_turn(h, pair, first_on_scalar):
            banks = []
            for g in range(2):
                bank = psum.tile([P, 2, 2, 128], F32, name="bank", tag=("bank", "plain")[h], bufs=4)
                banks.append(bank)
            for j in range(2):
                for g in range(2):
                    for u in range(2):
                        if h == 0:
                            words = qs[h][pair][:, j, :].bitcast(F32)[:, 256 * g + u : 256 * g + 256 : 2]
                        else:
                            words = qd[pair][:, j, :].bitcast(F32)[:, 256 * g + 128 * u : 256 * g + 128 * u + 128]
                        nc.tensor.transpose(banks[g][:, u, j, :], words, ident[:])
            for g in range(2):
                copy(
                    (g == 0) == first_on_scalar,
                    qt[h][:, g, :, 256 * pair : 256 * pair + 256],
                    banks[g][:].rearrange("p u j n -> p u (j n)"),
                )

        def qt_view(h, g, t):
            return qt[h][:, g, t // 2, :].bitcast(BF16)[:, t % 2 : 1024 : 2]

        def permute_words(g, eng, which):
            b = slice(1024 * g, 1024 * g + 1024)
            for src, dst in (((wl_w, wl_p), (wm_w, wm_p))[which],):
                eng.tensor_copy(
                    out=dst[:, b].rearrange("p (t m b) -> p t m b", t=4, b=2),
                    in_=src[:, b].rearrange("p (m t b) -> p t m b", t=4, b=2),
                )

        def permute_scales(g, eng, which):
            b = slice(512 * g, 512 * g + 512)
            for src, dst in (((wl_sr, wl_sp), (wm_sr, wm_sp))[which],):
                eng.tensor_copy(
                    out=dst[:, b].rearrange("p (t m) -> p t m", t=4),
                    in_=src[:, b].rearrange("p (m t) -> p t m", t=4),
                )

        units = [(0, 0), (0, 1), (1, 0), (1, 1)]
        st = {}

        def pl(u, t, n0=0, n1=512, between=()):
            h, g = units[u]
            bank = psum.tile([P, n1 - n0], F32, name="plain", tag="plain", bufs=4)
            st["pl", u, t, n0] = bank
            for gk in range(2):
                for tk in range(4):
                    nc.tensor.matmul(
                        bank[:],
                        lhsT=wqs[g][:, gk, tk, t : 512 : 4],
                        rhs=qt_view(h, gk, tk)[:, n0:n1],
                        start=(gk == 0 and tk == 0),
                        stop=(gk == 1 and tk == 3),
                    )
                if gk == 0:
                    for f in between:
                        f()

        def keep_warm(count):
            for k in range(count):
                nc.tensor.matmul(warm_bank[:], lhsT=zero[:, 0:128], rhs=zero[:], start=True, stop=True)

        def mx1(u, t, wp, wsp, key):
            h, g = units[u]
            k = 4 * g + t
            bank = psum.tile([P, 512], F32, name="bank", tag="bank", bufs=4)
            st[key, u, t] = bank
            nc.tensor.matmul_mx(
                out=bank[:],
                lhsT=wp[:, 256 * k : 256 * k + 256].bitcast(FP4X4),
                lhsT_scale=wsp[:, 128 * k : 128 * k + 128],
                rhs=cq[h][:].bitcast(FP8X4),
                rhs_scale=cqs[h][:],
                start=True,
                stop=True,
            )

        def igq(u, t):
            h, g = units[u]
            z = work.tile([P, 512], F32, name="igqt", bufs=7)
            st["igq", u, t] = z
            nc.scalar.activation(
                out=z[:], in_=qt_view(h, g, t), func=IDENTITY,
                scale=igf[:, 4 * g + t : 4 * g + t + 1], bias=igh[:, 4 * g + t : 4 * g + t + 1],
            )

        def mx_pair(u, t):
            mx1(u, t, wl_p, wl_sp, "mxl")
            mx1(u, t, wm_p, wm_sp, "mxm")

        def a_op(u, t):
            z = work.tile([P, 512], F32, name="lmx", bufs=5)
            st["lmx", u, t] = z
            nc.scalar.copy(out=z[:], in_=st["mxl", u, t][:])

        def d_op(u, t):
            h, g = units[u]
            z = work.tile([P, 512], F32, name="wsum", bufs=7)
            st["w", u, t] = z
            if u == 3:
                nc.vector.scalar_tensor_tensor(
                    out=z[:], in0=st["mxm", u, t][:], scalar=igf[:, 4 * g + t : 4 * g + t + 1], in1=st["igq", u, t][:],
                    op0=MULT, op1=ADD,
                )
            else:
                nc.vector.scalar_tensor_tensor(
                    out=z[:], in0=st["mxm", u, t][:], scalar=-0.5, in1=qt_view(h, g, t), op0=ADD, op1=ADD,
                )

        def b_op(u, t, n0=0, n1=512):
            z = work.tile([P, n1 - n0], F32, name="lsum", bufs=3)
            st["ls", u, t, n0] = z
            nc.vector.tensor_tensor(out=z[:], in0=st["pl", u, t, n0][:], in1=st["lmx", u, t][:, n0:n1], op=ADD)

        def c_op(u, t, n0=0, n1=512):
            z = work.tile([P, n1 - n0], F32, name="th", bufs=5)
            st["th", u, t, n0] = z
            nc.scalar.activation(out=z[:], in_=st["ls", u, t, n0][:], func=SIGMOID, scale=2.0)

        def e_op(u, t, n0=0, n1=512):
            g = units[u][1]
            if u == 3:
                if t == 0 and n0 == 0:
                    ye = work.tile([P, 4, 512], BF16, name="ye", bufs=2)
                    st["ye", u] = ye
                nc.vector.scalar_tensor_tensor(
                    out=st["ye", u][:, t, n0:n1], in0=st["th", u, t, n0][:], scalar=igf[:, 4 * g + t : 4 * g + t + 1],
                    in1=st["w", u, t][:, n0:n1], op0=MULT, op1=ADD,
                )
            else:
                z = work.tile([P, 512], F32, name="ysum", bufs=6)
                st["y", u, t] = z
                nc.gpsimd.tensor_tensor(out=z[:], in0=st["th", u, t, 0][:], in1=st["w", u, t][:], op=ADD)

        def x_op(u, t):
            g = units[u][1]
            if t == 0:
                ye = work.tile([P, 4, 512], BF16, name="ye", bufs=2)
                st["ye", u] = ye
            nc.scalar.activation(
                out=st["ye", u][:, t, :], in_=st["y", u, t][:], func=COPY, scale=igf[:, 4 * g + t : 4 * g + t + 1]
            )

        def f_op(u, n0, n1):
            if n0 == 0:
                yi = work.tile([P, 512, 4], BF16, name="yi", bufs=2, align_bytes=64)
                st["yi", u] = yi
            nc.vector.tensor_copy(
                out=st["yi", u][:, n0:n1, :], in_=st["ye", u][:, :, n0:n1].rearrange("p t n -> p n t")
            )

        def q_op(u, n0, n1):
            h, g = units[u]
            nc.vector.quantize_mx(
                out=yq[h][:, g, n0:n1].bitcast(FP8X4),
                scales=yqs[h][:, g, n0:n1],
                in_=st["yi", u][:, n0:n1, :].rearrange("p n t -> p (n t)"),
            )

        out_v = out.rearrange("(p i) o -> p i o", i=8)

        def st2(h, i, o):
            bank = psum.tile([P, 512], F32, name="bank", tag="bank", bufs=4)
            st["o", h, i, o] = bank
            for g in range(2):
                nc.tensor.matmul_mx(
                    out=bank[:],
                    lhsT=yq[h][:, g, 128 * i : 128 * i + 128].bitcast(FP8X4),
                    lhsT_scale=yqs[h][:, g, 128 * i : 128 * i + 128],
                    rhs=ws_w[:, g, 1024 * o : 1024 * o + 1024].bitcast(FP4X4),
                    rhs_scale=ws_s[:, g, 512 * o : 512 * o + 512],
                    start=(g == 0),
                    stop=(g == 1),
                )

        def o_op(h, i, o, on_scalar):
            ot = work.tile([P, 512], F32, name="ot", bufs=10)
            copy(on_scalar, ot[:], st["o", h, i, o][:])
            nc.sync.dma_start(out=out_v[:, 4 * h + i, 512 * o : 512 * o + 512], in_=ot[:])

        warm_bank = psum.tile([P, 512], F32, name="warm_bank", tag="plain", bufs=4)
        keep_warm(5)
        q_turn(0, 0, False)
        keep_warm(2)
        q_turn(0, 1, False)
        keep_warm(1)
        pl(0, 0)
        permute_scales(0, nc.vector, 0)
        widen(0, 0, False)
        widen(0, 1, False)
        widen(0, 3, True)
        widen(0, 2, False, (0, 1))
        widen(0, 2, True, (2, 3))
        pl(0, 1)
        permute_words(0, nc.vector, 0)
        nc.vector.tensor_copy(out=igf[:], in_=igb[:])
        nc.vector.tensor_scalar(out=igh[:], in0=igb[:], scalar1=-0.5, scalar2=None, op0=MULT)
        permute_words(0, nc.gpsimd, 1)
        permute_scales(1, nc.gpsimd, 0)
        permute_scales(1, nc.gpsimd, 1)
        c_turn(0, 0, False)
        c_turn(0, 1, True)
        c_quant(0)
        permute_scales(0, nc.vector, 1)
        widen(1, 0, False)
        pl(0, 2)
        seq = [(u, t) for u in range(3) for t in range(4)] + [(3, 0), (3, 1), (3, 2), (3, 3)]
        extra = {
            (1, 1): [lambda: c_turn(1, 0, False), lambda: c_turn(1, 1, True)],
            (1, 2): [lambda: c_quant(1), lambda: q_turn(1, 0, False)],
            (1, 3): [lambda: q_turn(1, 1, False)],
            (1, 0): [],
        }
        late = {
            (2, 0): [lambda: f_op(0, 0, 512), lambda: q_op(0, 0, 512)],
            (2, 2): [lambda: f_op(1, 0, 512), lambda: q_op(1, 0, 512)],
            (3, 2): [lambda: f_op(2, 0, 256)],
            (3, 3): [lambda: f_op(2, 256, 512), lambda: q_op(2, 0, 512)],
        }
        x_at = {5: [0], 6: [1, 2], 7: [3, 4], 8: [5, 6], 9: [7], 10: [8], 11: [9], 12: [10], 13: [11]}
        for s, (u, t) in enumerate(seq):
            if s == 2:
                pl(0, 3)
            if s == 4:
                pl(u, t)
            mx_pair(u, t)
            a_op(u, t)
            if u == 3:
                st2(0, t // 2, t % 2)
            if u == 3:
                pl(3, t, 0, 256)
            elif s > 4:
                pl(u, t, 0, 512, extra.get((u, t), []))
            if s:
                pu, pt = seq[s - 1]
                n1 = 256 if pu == 3 else 512
                b_op(pu, pt, 0, n1)
                c_op(pu, pt, 0, n1)
            d_op(u, t)
            if s:
                e_op(pu, pt, 0, n1)
            for k in x_at.get(s, []):
                x_op(*seq[k])
            if s == 1:
                permute_words(1, nc.vector, 0)
                widen(1, 1, True)
            if s == 2:
                permute_words(1, nc.vector, 1)
            if s == 3:
                widen(1, 2, True)
                widen(1, 3, False)
            if s == 4:
                q_sort(0)
            if s == 5:
                q_sort(1)
            if u == 2:
                igq(3, t)
            if u == 3:
                o_op(0, t // 2, t % 2, t % 2 == 1)
            for f in late.get((u, t), []):
                f()
        pl(3, 0, 256, 512)
        b_op(3, 3, 0, 256)
        c_op(3, 3, 0, 256)
        st2(0, 2, 0)
        o_op(0, 2, 0, True)
        pl(3, 1, 256, 512)
        b_op(3, 0, 256, 512)
        e_op(3, 3, 0, 256)
        c_op(3, 0, 256, 512)
        f_op(3, 0, 256)
        st2(0, 2, 1)
        o_op(0, 2, 1, True)
        pl(3, 2, 256, 512)
        b_op(3, 1, 256, 512)
        c_op(3, 1, 256, 512)
        e_op(3, 0, 256, 512)
        q_op(3, 0, 256)
        st2(0, 3, 0)
        pl(3, 3, 256, 512)
        b_op(3, 2, 256, 512)
        c_op(3, 2, 256, 512)
        e_op(3, 1, 256, 512)
        o_op(0, 3, 0, False)
        st2(0, 3, 1)
        o_op(0, 3, 1, True)
        b_op(3, 3, 256, 512)
        c_op(3, 3, 256, 512)
        e_op(3, 2, 256, 512)
        e_op(3, 3, 256, 512)
        for i in (0, 1):
            for o in (0, 1):
                st2(1, i, o)
                o_op(1, i, o, True)
        for i in (2, 3):
            f_op(3, 128 * i, 128 * i + 128)
            q_op(3, 128 * i, 128 * i + 128)
            for o in (0, 1):
                st2(1, i, o)
        for i in (2, 3):
            for o in (0, 1):
                o_op(1, i, o, o == 1)
